import numpy as np
import ml_dtypes


def mxq(x, axis, fmt="e4m3"):
    dtype, down = {"e4m3": (ml_dtypes.float8_e4m3fn, 7), "e5m2": (ml_dtypes.float8_e5m2, 14)}[fmt]
    v = np.moveaxis(np.asarray(x, np.float32).astype(ml_dtypes.bfloat16).astype(np.float64), axis, -1)
    blocks = v.reshape(v.shape[:-1] + (-1, 32))
    amax = np.abs(blocks).max(-1, keepdims=True)
    byte = np.maximum(np.where(amax > 0, np.frexp(amax)[1] - 1 + 127, 0) - down, 1)
    scale = np.exp2(byte - 127.0)
    codes = (blocks / scale).astype(np.float32).astype(dtype).astype(np.float64)
    return np.moveaxis((codes * scale).reshape(v.shape), -1, axis)


WIDE = False


def mx_kscale(k, group=512):
    if not WIDE:
        return np.ones(k)
    levels = np.array([10, -10, 5, -5, 0])
    if group != 512:
        return np.exp2(np.random.permutation(np.resize(levels, k // group))).repeat(group)
    if k % 512:
        return np.exp2(np.random.permutation(np.resize(levels, k // 32))).repeat(32)
    a = np.empty((k // 512, 16))
    for p in range(k // 512):
        a[p, :8] = np.random.permutation(np.resize(levels, 8))
        for g in range(8):
            far = levels[np.abs(levels - a[p, g]) >= 10]
            a[p, g + 8] = far[np.random.randint(len(far))]
    return np.exp2(a.ravel()).repeat(32)


def f64(x):
    return np.asarray(x).astype(np.float64)


def bf(x):
    return np.asarray(x, np.float32).astype(ml_dtypes.bfloat16)


def planes(Y):
    r, m = Y.shape
    b = f64(bf(Y)).reshape(r // 32, 32, m)
    amax = np.abs(b).max(1)
    byte = np.clip(np.where(amax > 0, np.frexp(amax)[1] - 1 + 127 - 7, 1), 1, 254)
    codes = (b * np.exp2(127.0 - byte)[:, None, :]).reshape(r, m).astype(np.float32).astype(ml_dtypes.float8_e4m3fn).view(np.uint8)
    words = codes.reshape(r // 512, 128, 4, m).transpose(0, 1, 3, 2)
    return np.ascontiguousarray(words), np.ascontiguousarray(byte.astype(np.uint8).reshape(r // 512, 16, m))


G, D, M, N = 2, 256, 256, 512


def setup_inputs():
    n = np.random.standard_normal
    s_d = mx_kscale(D, 0)
    return {
        "x": (n((G, D, N)) * s_d[:, None]).astype(np.float32),
        "fc": (np.cos(2 * np.pi * np.outer(np.arange(D), np.arange(M)) / D) * (2 / np.sqrt(D)) / s_d[:, None]).astype(np.float32),
        "fs": (np.sin(2 * np.pi * (np.outer(np.arange(D), np.arange(M)) + 0.25) / D) * (2 / np.sqrt(D)) / s_d[:, None]).astype(np.float32),
    }


def reference(x, fc, fs):
    fcq = mxq(f64(fc), 0, "e4m3")
    xq = mxq(f64(x), 1, "e4m3")
    re = fcq.T @ xq
    fsq = mxq(f64(fs), 0, "e4m3")
    im = fsq.T @ xq
    y = np.square(re) + np.square(im)
    Y = y.reshape(G * M, N)
    words, scales = planes(Y)
    return Y, words, scales

@@ -1,0 +1,157 @@
+from contextlib import ExitStack
+
+import concourse.mybir as mybir
+
+G, D, M, N = 2, 256, 256, 512
+FLOPS = 2 * 2 * G * D * M * N
+
+F32 = mybir.dt.float32
+BF16 = mybir.dt.bfloat16
+I32 = mybir.dt.int32
+U32 = mybir.dt.uint32
+U8 = mybir.dt.uint8
+FP8X4 = mybir.dt.float8_e4m3fn_x4
+ACT = mybir.ActivationFunctionType
+ADD = mybir.AluOpType.add
+
+P = 128
+ROWS = 64
+PACK = 4
+COLS = 128
+STEPS = 2
+BLOCKS = 2 * PACK + 1
+CODE_BYTES = BLOCKS * ROWS * 4
+SCALE_BYTES = BLOCKS * ROWS
+F_SPLIT = 40
+
+
+def tile_rows_pl_dft_pow_kernel(tc, x, fc, fs, out_0, out_1, out_2):
+    nc = tc.nc
+    y_hbm = out_0.rearrange("(g p u) n -> g p u n", g=G, u=PACK)
+    words_hbm = out_1.rearrange("v p n b -> (v p) (n b)").bitcast(I32).rearrange("(g p) n -> p g n", g=G)
+    scales_hbm = out_2.rearrange("v f n -> (v f) n").bitcast(I32).rearrange("(g a r) w -> a r g w", g=G, a=2)
+    x_hbm = x.rearrange("g (p j) n -> (g p) j n", j=PACK)
+
+    with ExitStack() as ctx:
+        sb = ctx.enter_context(tc.tile_pool(name="sb", bufs=1))
+        ps = ctx.enter_context(tc.psum_pool(name="ps", bufs=1))
+        ctx.enter_context(tc.manual_schedule())
+
+        f_raw = sb.tile([P, PACK, M], F32, name="f_raw", align_bytes=64)
+        nc.sync.dma_start(out=f_raw[0:ROWS], in_=fc.rearrange("(p j) m -> p j m", j=PACK))
+        nc.scalar.dma_start(out=f_raw[ROWS:P], in_=fs.rearrange("(p j) m -> p j m", j=PACK))
+        x_raw = []
+        for s in range(STEPS):
+            raw = sb.tile([P, PACK, 2 * COLS], F32, name="x_raw%d" % s, align_bytes=64)
+            nc.sync.dma_start(out=raw[:], in_=x_hbm[:, :, 2 * COLS * s : 2 * COLS * (s + 1)])
+            x_raw.append(raw)
+
+        own = sb.tile([P, CODE_BYTES + SCALE_BYTES], U8, name="own", align_bytes=64)
+        swapped = sb.tile([P, CODE_BYTES + SCALE_BYTES], U8, name="swapped", align_bytes=64)
+        nc.vector.memset(own[:].bitcast(I32), 0)
+
+        def window(weights, block, blocks):
+            codes = weights[:, 4 * ROWS * block : 4 * ROWS * (block + blocks)]
+            scales = weights[:, CODE_BYTES + ROWS * block : CODE_BYTES + ROWS * (block + blocks)]
+            return codes, scales
+
+        f_bf = sb.tile([P, PACK, ROWS, PACK], BF16, name="f_bf", align_bytes=64)
+        f_out = f_bf[:].rearrange("p u m j -> p m u j")
+        f_in = f_raw[:].rearrange("p j (m u) -> p m u j", u=PACK)
+        nc.vector.tensor_copy(out=f_out[:, 0:F_SPLIT], in_=f_in[:, 0:F_SPLIT])
+        nc.scalar.activation(out=f_out[:, F_SPLIT:ROWS], in_=f_in[:, F_SPLIT:ROWS], func=ACT.Copy)
+        for u in range(PACK):
+            codes, scales = window(own, 2 * u + 1, 1)
+            nc.vector.quantize_mx(
+                out=codes.bitcast(FP8X4), scales=scales, in_=f_bf[:, u].rearrange("p m j -> p (m j)")
+            )
+        nc.sync.dma_start(out=swapped[ROWS:P, :].bitcast(I32), in_=own[0:ROWS, :].bitcast(I32))
+        nc.sync.dma_start(out=swapped[0:ROWS, :].bitcast(I32), in_=own[ROWS:P, :].bitcast(I32))
+
+        def interleave(copy, dst, src):
+            copy(dst.rearrange("p (c i) t -> p c t i", i=4), src.rearrange("p t (c i) -> p c t i", i=4))
+
+        def on_vector(dst, src):
+            nc.vector.tensor_copy(out=dst, in_=src)
+
+        def on_scalar(dst, src):
+            nc.scalar.activation(out=dst, in_=src, func=ACT.Copy)
+
+        x_codes, x_scales = {}, {}
+        for s in range(STEPS):
+            x_bf = []
+            for h in range(2):
+                bf = sb.tile([P, COLS, PACK], BF16, name="x_bf%d%d" % (s, h), align_bytes=64)
+                interleave(on_vector if h == 0 else on_scalar, bf[:], x_raw[s][:, :, COLS * h : COLS * (h + 1)])
+                x_bf.append(bf)
+            for h in range(2):
+                x_codes[s, h] = sb.tile([P, COLS], U32, name="x_codes%d%d" % (s, h), align_bytes=64)
+                x_scales[s, h] = sb.tile([P, COLS], U8, name="x_scales%d%d" % (s, h), align_bytes=64)
+                nc.vector.quantize_mx(
+                    out=x_codes[s, h][:].bitcast(FP8X4),
+                    scales=x_scales[s, h][:],
+                    in_=x_bf[h][:].rearrange("p n j -> p (n j)"),
+                )
+
+        banks = {}
+        for s in range(STEPS):
+            for k, weights in enumerate((own, swapped)):
+                for g in range(G):
+                    banks[s, k, g] = ps.tile([P, PACK, COLS], F32, name="bank%d%d%d" % (s, k, g))
+                for u in range(PACK):
+                    for h in range(2):
+                        codes, scales = window(weights, 2 * u + 1 - h, 2)
+                        for g in range(G):
+                            rows = slice(ROWS * g, ROWS * (g + 1))
+                            nc.tensor.matmul_mx(
+                                out=banks[s, k, g][:, u, :],
+                                lhsT=codes[rows].bitcast(FP8X4),
+                                lhsT_scale=scales[rows],
+                                rhs=x_codes[s, h][rows, :].bitcast(FP8X4),
+                                rhs_scale=x_scales[s, h][rows, :],
+                                start=(h == 0),
+                                stop=(h == 1),
+                            )
+
+        for s in range(STEPS):
+            squares = {}
+            for k in range(2):
+                for g in range(G):
+                    squares[k, g] = sb.tile([P, PACK, COLS], F32, name="sq%d%d%d" % (s, k, g), align_bytes=64)
+                    nc.scalar.activation(out=squares[k, g][:], in_=banks[s, k, g][:], func=ACT.Square)
+            words = sb.tile([P, G, COLS], U32, name="words%d" % s, align_bytes=64)
+            scales = sb.tile([P, G, COLS], U8, name="scales%d" % s, align_bytes=64)
+            last = s == STEPS - 1
+            queues = (nc.sync, nc.scalar if last else nc.sync)
+            ys, y_bf = [], []
+            for g in range(G):
+                y = sb.tile([P, PACK, COLS], F32, name="y%d%d" % (s, g), align_bytes=64)
+                nc.vector.tensor_tensor(out=y[:], in0=squares[0, g][:], in1=squares[1, g][:], op=ADD)
+                ys.append(y)
+            for g in range(G):
+                for h in range(2):
+                    q = 2 * s + h
+                    queues[h].dma_start(
+                        out=y_hbm[g][:, :, COLS * q : COLS * (q + 1)], in_=ys[g][ROWS * h : ROWS * (h + 1)]
+                    )
+                bf = sb.tile([P, COLS, PACK], BF16, name="y_bf%d%d" % (s, g), align_bytes=64)
+                interleave(on_scalar if last and g == 0 else on_vector, bf[:], ys[g][:])
+                y_bf.append(bf)
+            for g in range(G):
+                nc.vector.quantize_mx(
+                    out=words[:, g, :].bitcast(FP8X4),
+                    scales=scales[:, g, :],
+                    in_=y_bf[g][:].rearrange("p n u -> p (n u)"),
+                )
+            for h in range(2):
+                q = 2 * s + h
+                queues[h].dma_start(
+                    out=words_hbm[:, :, COLS * q : COLS * (q + 1)],
+                    in_=words[ROWS * h : ROWS * (h + 1)].bitcast(I32),
+                )
+                for a in range(2):
+                    first = ROWS * h + 32 * a
+                    queues[h].dma_start(
+                        out=scales_hbm[a][:, :, 32 * q : 32 * (q + 1)],
+                        in_=scales[first : first + 4].bitcast(I32),
+                    )

@@ -19,10 +19,12 @@ ROWS = 64
 PACK = 4
 COLS = 128
 STEPS = 2
-BLOCKS = 2 * PACK + 1
+BLOCKS = PACK + 1
 CODE_BYTES = BLOCKS * ROWS * 4
 SCALE_BYTES = BLOCKS * ROWS
 F_SPLIT = 40
+WARM_EARLY = 34
+WARM_LATE = 8
 
 
 def tile_rows_pl_dft_pow_kernel(tc, x, fc, fs, out_0, out_1, out_2):
@@ -30,7 +32,7 @@ def tile_rows_pl_dft_pow_kernel(tc, x, fc, fs, out_0, out_1, out_2):
     y_hbm = out_0.rearrange("(g p u) n -> g p u n", g=G, u=PACK)
     words_hbm = out_1.rearrange("v p n b -> (v p) (n b)").bitcast(I32).rearrange("(g p) n -> p g n", g=G)
     scales_hbm = out_2.rearrange("v f n -> (v f) n").bitcast(I32).rearrange("(g a r) w -> a r g w", g=G, a=2)
-    x_hbm = x.rearrange("g (p j) n -> (g p) j n", j=PACK)
+    x_hbm = x.rearrange("g (p j) (h s c) -> s (g p) (j h) c", j=PACK, h=2, s=STEPS)
 
     with ExitStack() as ctx:
         sb = ctx.enter_context(tc.tile_pool(name="sb", bufs=1))
@@ -42,18 +44,44 @@ def tile_rows_pl_dft_pow_kernel(tc, x, fc, fs, out_0, out_1, out_2):
         nc.scalar.dma_start(out=f_raw[ROWS:P], in_=fs.rearrange("(p j) m -> p j m", j=PACK))
         x_raw = []
         for s in range(STEPS):
-            raw = sb.tile([P, PACK, 2 * COLS], F32, name="x_raw%d" % s, align_bytes=64)
-            nc.sync.dma_start(out=raw[:], in_=x_hbm[:, :, 2 * COLS * s : 2 * COLS * (s + 1)])
+            raw = sb.tile([P, PACK, 2, COLS], F32, name="x_raw%d" % s, align_bytes=64)
+            nc.sync.dma_start(out=raw[:].rearrange("p j h c -> p (j h) c"), in_=x_hbm[s])
             x_raw.append(raw)
 
-        own = sb.tile([P, CODE_BYTES + SCALE_BYTES], U8, name="own", align_bytes=64)
-        swapped = sb.tile([P, CODE_BYTES + SCALE_BYTES], U8, name="swapped", align_bytes=64)
-        nc.vector.memset(own[:].bitcast(I32), 0)
+        own, swapped = [], []
+        for v in range(2):
+            own.append(sb.tile([P, CODE_BYTES + SCALE_BYTES], U8, name="own%d" % v, align_bytes=64))
+            swapped.append(sb.tile([P, CODE_BYTES + SCALE_BYTES], U8, name="swapped%d" % v, align_bytes=64))
+
+        zero_bf = sb.tile([P, PACK * COLS], BF16, name="zero_bf", align_bytes=64)
+        zero_codes = sb.tile([P, COLS], U32, name="zero_codes", align_bytes=64)
+        zero_scales = sb.tile([P, COLS], U8, name="zero_scales", align_bytes=64)
+        warm_bank = ps.tile([P, COLS], F32, name="warm_bank")
+
+        def warm(count, codes, scales):
+            for i in range(count):
+                nc.tensor.matmul_mx(
+                    out=warm_bank[:],
+                    lhsT=codes.bitcast(FP8X4),
+                    lhsT_scale=scales,
+                    rhs=zero_codes[:].bitcast(FP8X4),
+                    rhs_scale=zero_scales[:],
+                    start=True,
+                    stop=True,
+                )
 
         def window(weights, block, blocks):
             codes = weights[:, 4 * ROWS * block : 4 * ROWS * (block + blocks)]
             scales = weights[:, CODE_BYTES + ROWS * block : CODE_BYTES + ROWS * (block + blocks)]
             return codes, scales
+
+        nc.vector.memset(zero_bf[:], 0.0)
+        table = sb.tile([P, 1], F32, name="table")
+        nc.scalar.activation(out=table[:], in_=zero_bf[:, 0:1], func=ACT.Square)
+        nc.vector.quantize_mx(out=zero_codes[:].bitcast(FP8X4), scales=zero_scales[:], in_=zero_bf[:])
+        for v in range(2):
+            nc.vector.memset(own[v][:].bitcast(I32), 0)
+        warm(WARM_EARLY, zero_codes[:], zero_scales[:])
 
         f_bf = sb.tile([P, PACK, ROWS, PACK], BF16, name="f_bf", align_bytes=64)
         f_out = f_bf[:].rearrange("p u m j -> p m u j")
@@ -61,12 +89,14 @@ def tile_rows_pl_dft_pow_kernel(tc, x, fc, fs, out_0, out_1, out_2):
         nc.vector.tensor_copy(out=f_out[:, 0:F_SPLIT], in_=f_in[:, 0:F_SPLIT])
         nc.scalar.activation(out=f_out[:, F_SPLIT:ROWS], in_=f_in[:, F_SPLIT:ROWS], func=ACT.Copy)
         for u in range(PACK):
-            codes, scales = window(own, 2 * u + 1, 1)
+            codes, scales = window(own[u // 2], 2 * (u % 2) + 1, 1)
             nc.vector.quantize_mx(
                 out=codes.bitcast(FP8X4), scales=scales, in_=f_bf[:, u].rearrange("p m j -> p (m j)")
             )
-        nc.sync.dma_start(out=swapped[ROWS:P, :].bitcast(I32), in_=own[0:ROWS, :].bitcast(I32))
-        nc.sync.dma_start(out=swapped[0:ROWS, :].bitcast(I32), in_=own[ROWS:P, :].bitcast(I32))
+        warm(WARM_LATE, *window(own[0], 0, 2))
+        for v in range(2):
+            nc.sync.dma_start(out=swapped[v][0:ROWS, :].bitcast(I32), in_=own[v][ROWS:P, :].bitcast(I32))
+            nc.sync.dma_start(out=swapped[v][ROWS:P, :].bitcast(I32), in_=own[v][0:ROWS, :].bitcast(I32))
 
         def interleave(copy, dst, src):
             copy(dst.rearrange("p (c i) t -> p c t i", i=4), src.rearrange("p t (c i) -> p c t i", i=4))
@@ -82,7 +112,7 @@ def tile_rows_pl_dft_pow_kernel(tc, x, fc, fs, out_0, out_1, out_2):
             x_bf = []
             for h in range(2):
                 bf = sb.tile([P, COLS, PACK], BF16, name="x_bf%d%d" % (s, h), align_bytes=64)
-                interleave(on_vector if h == 0 else on_scalar, bf[:], x_raw[s][:, :, COLS * h : COLS * (h + 1)])
+                interleave(on_vector if h == 0 else on_scalar, bf[:], x_raw[s][:, :, h, :])
                 x_bf.append(bf)
             for h in range(2):
                 x_codes[s, h] = sb.tile([P, COLS], U32, name="x_codes%d%d" % (s, h), align_bytes=64)
@@ -95,63 +125,119 @@ def tile_rows_pl_dft_pow_kernel(tc, x, fc, fs, out_0, out_1, out_2):
 
         banks = {}
         for s in range(STEPS):
-            for k, weights in enumerate((own, swapped)):
-                for g in range(G):
-                    banks[s, k, g] = ps.tile([P, PACK, COLS], F32, name="bank%d%d%d" % (s, k, g))
-                for u in range(PACK):
-                    for h in range(2):
-                        codes, scales = window(weights, 2 * u + 1 - h, 2)
-                        for g in range(G):
-                            rows = slice(ROWS * g, ROWS * (g + 1))
-                            nc.tensor.matmul_mx(
-                                out=banks[s, k, g][:, u, :],
-                                lhsT=codes[rows].bitcast(FP8X4),
-                                lhsT_scale=scales[rows],
-                                rhs=x_codes[s, h][rows, :].bitcast(FP8X4),
-                                rhs_scale=x_scales[s, h][rows, :],
-                                start=(h == 0),
-                                stop=(h == 1),
-                            )
-
-        for s in range(STEPS):
-            squares = {}
             for k in range(2):
                 for g in range(G):
-                    squares[k, g] = sb.tile([P, PACK, COLS], F32, name="sq%d%d%d" % (s, k, g), align_bytes=64)
-                    nc.scalar.activation(out=squares[k, g][:], in_=banks[s, k, g][:], func=ACT.Square)
-            words = sb.tile([P, G, COLS], U32, name="words%d" % s, align_bytes=64)
-            scales = sb.tile([P, G, COLS], U8, name="scales%d" % s, align_bytes=64)
-            last = s == STEPS - 1
-            queues = (nc.sync, nc.scalar if last else nc.sync)
-            ys, y_bf = [], []
+                    if (s, k, g) == (1, 1, 1):
+                        banks[s, k, g] = banks[0, 0, 1]
+                    else:
+                        banks[s, k, g] = ps.tile([P, PACK, COLS], F32, name="bank%d%d%d" % (s, k, g))
+
+        def multiply(s, g, i):
+            k, u, h = i // 8, i // 2 % 4, i % 2
+            codes, scales = window((own, swapped)[k][u // 2], 2 * (u % 2) + 1 - h, 2)
+            rows = slice(ROWS * g, ROWS * (g + 1))
+            nc.tensor.matmul_mx(
+                out=banks[s, k, g][:, u, :],
+                lhsT=codes[rows].bitcast(FP8X4),
+                lhsT_scale=scales[rows],
+                rhs=x_codes[s, h][rows, :].bitcast(FP8X4),
+                rhs_scale=x_scales[s, h][rows, :],
+                start=(h == 0),
+                stop=(h == 1),
+            )
+
+        def paired(s):
+            for i in range(16):
+                multiply(s, 0, i)
+                multiply(s, 1, i)
+
+        def leading(s):
+            for i in range(8):
+                multiply(s, 0, 2 * i)
+                multiply(s, 1, i)
+                multiply(s, 0, 2 * i + 1)
+            for i in range(8, 16):
+                multiply(s, 1, i)
+
+        squares, ys, y_bf = {}, {}, {}
+        words = sb.tile([P, G, STEPS * COLS], U32, name="words", align_bytes=64)
+        scales = sb.tile([P, G, STEPS * COLS], U8, name="scales", align_bytes=64)
+        for s in range(STEPS):
             for g in range(G):
-                y = sb.tile([P, PACK, COLS], F32, name="y%d%d" % (s, g), align_bytes=64)
-                nc.vector.tensor_tensor(out=y[:], in0=squares[0, g][:], in1=squares[1, g][:], op=ADD)
-                ys.append(y)
-            for g in range(G):
-                for h in range(2):
-                    q = 2 * s + h
-                    queues[h].dma_start(
-                        out=y_hbm[g][:, :, COLS * q : COLS * (q + 1)], in_=ys[g][ROWS * h : ROWS * (h + 1)]
-                    )
-                bf = sb.tile([P, COLS, PACK], BF16, name="y_bf%d%d" % (s, g), align_bytes=64)
-                interleave(on_scalar if last and g == 0 else on_vector, bf[:], ys[g][:])
-                y_bf.append(bf)
-            for g in range(G):
-                nc.vector.quantize_mx(
-                    out=words[:, g, :].bitcast(FP8X4),
-                    scales=scales[:, g, :],
-                    in_=y_bf[g][:].rearrange("p n u -> p (n u)"),
+                ys[s, g] = sb.tile([P, PACK, COLS], F32, name="y%d%d" % (s, g), align_bytes=64)
+                y_bf[s, g] = sb.tile([P, COLS, PACK], BF16, name="y_bf%d%d" % (s, g), align_bytes=64)
+                for k in range(2):
+                    squares[s, k, g] = sb.tile([P, PACK, COLS], F32, name="sq%d%d%d" % (s, k, g), align_bytes=64)
+
+        whole = slice(0, COLS)
+        left, right = slice(0, COLS // 2), slice(COLS // 2, COLS)
+
+        def square(s, k, g, cols=whole):
+            nc.scalar.activation(out=squares[s, k, g][:, :, cols], in_=banks[s, k, g][:, :, cols], func=ACT.Square)
+
+        def add(s, g, cols=whole):
+            nc.vector.tensor_tensor(
+                out=ys[s, g][:, :, cols], in0=squares[s, 0, g][:, :, cols], in1=squares[s, 1, g][:, :, cols], op=ADD
+            )
+
+        def regroup(s, g, copy=on_vector, cols=whole):
+            interleave(copy, y_bf[s, g][:, cols, :], ys[s, g][:, :, cols])
+
+        def quantize(s, g):
+            nc.vector.quantize_mx(
+                out=words[:, g, COLS * s : COLS * (s + 1)].bitcast(FP8X4),
+                scales=scales[:, g, COLS * s : COLS * (s + 1)],
+                in_=y_bf[s, g][:].rearrange("p n u -> p (n u)"),
+            )
+
+        def store_y(s, g, h, queue):
+            q = 2 * h + s
+            queue.dma_start(out=y_hbm[g][:, :, COLS * q : COLS * (q + 1)], in_=ys[s, g][ROWS * h : ROWS * (h + 1)])
+
+        def store_planes(h, queue):
+            queue.dma_start(
+                out=words_hbm[:, :, 2 * COLS * h : 2 * COLS * (h + 1)],
+                in_=words[ROWS * h : ROWS * (h + 1)].bitcast(I32),
+            )
+            for a in range(2):
+                first = ROWS * h + 32 * a
+                queue.dma_start(
+                    out=scales_hbm[a][:, :, 64 * h : 64 * (h + 1)],
+                    in_=scales[first : first + 4].bitcast(I32),
                 )
-            for h in range(2):
-                q = 2 * s + h
-                queues[h].dma_start(
-                    out=words_hbm[:, :, COLS * q : COLS * (q + 1)],
-                    in_=words[ROWS * h : ROWS * (h + 1)].bitcast(I32),
-                )
-                for a in range(2):
-                    first = ROWS * h + 32 * a
-                    queues[h].dma_start(
-                        out=scales_hbm[a][:, :, 32 * q : 32 * (q + 1)],
-                        in_=scales[first : first + 4].bitcast(I32),
-                    )
+
+        leading(0)
+        square(0, 0, 0)
+        square(0, 1, 0)
+        square(0, 0, 1)
+        add(0, 0)
+        store_y(0, 0, 0, nc.sync)
+        store_y(0, 0, 1, nc.sync)
+        square(0, 1, 1)
+        leading(1)
+        regroup(0, 0)
+        add(0, 1)
+        store_y(0, 1, 0, nc.sync)
+        store_y(0, 1, 1, nc.sync)
+        quantize(0, 0)
+        regroup(0, 1)
+        square(1, 0, 0)
+        square(1, 1, 0)
+        add(1, 0)
+        quantize(0, 1)
+        store_y(1, 0, 0, nc.sync)
+        store_y(1, 0, 1, nc.sync)
+        square(1, 0, 1)
+        square(1, 1, 1, left)
+        square(1, 1, 1, right)
+        regroup(1, 0, on_scalar)
+        add(1, 1, left)
+        add(1, 1, right)
+        regroup(1, 1, on_vector, left)
+        regroup(1, 1, on_vector, right)
+        store_y(1, 1, 0, nc.sync)
+        store_y(1, 1, 1, nc.scalar)
+        quantize(1, 0)
+        quantize(1, 1)
+        store_planes(0, nc.sync)
+        store_planes(1, nc.scalar)

@@ -19,11 +19,13 @@ ROWS = 64
 PACK = 4
 COLS = 128
 STEPS = 2
-BLOCKS = PACK + 1
-CODE_BYTES = BLOCKS * ROWS * 4
-SCALE_BYTES = BLOCKS * ROWS
+BLOCK_BYTES = 4 * ROWS
+SCALE_START = (2 * PACK + 1) * BLOCK_BYTES
+WEIGHT_BYTES = SCALE_START + 2 * BLOCK_BYTES
 F_SPLIT = 40
-WARM_EARLY = 34
+X_SPLIT = 88
+BANKS = 3
+WARM_EARLY = 26
 WARM_LATE = 8
 
 
@@ -32,7 +34,7 @@ def tile_rows_pl_dft_pow_kernel(tc, x, fc, fs, out_0, out_1, out_2):
     y_hbm = out_0.rearrange("(g p u) n -> g p u n", g=G, u=PACK)
     words_hbm = out_1.rearrange("v p n b -> (v p) (n b)").bitcast(I32).rearrange("(g p) n -> p g n", g=G)
     scales_hbm = out_2.rearrange("v f n -> (v f) n").bitcast(I32).rearrange("(g a r) w -> a r g w", g=G, a=2)
-    x_hbm = x.rearrange("g (p j) (h s c) -> s (g p) (j h) c", j=PACK, h=2, s=STEPS)
+    x_hbm = x.rearrange("g (p j) (h s c) -> s h (g p) j c", j=PACK, h=2, s=STEPS)
 
     with ExitStack() as ctx:
         sb = ctx.enter_context(tc.tile_pool(name="sb", bufs=1))
@@ -42,16 +44,14 @@ def tile_rows_pl_dft_pow_kernel(tc, x, fc, fs, out_0, out_1, out_2):
         f_raw = sb.tile([P, PACK, M], F32, name="f_raw", align_bytes=64)
         nc.sync.dma_start(out=f_raw[0:ROWS], in_=fc.rearrange("(p j) m -> p j m", j=PACK))
         nc.scalar.dma_start(out=f_raw[ROWS:P], in_=fs.rearrange("(p j) m -> p j m", j=PACK))
-        x_raw = []
+        x_raw = {}
         for s in range(STEPS):
-            raw = sb.tile([P, PACK, 2, COLS], F32, name="x_raw%d" % s, align_bytes=64)
-            nc.sync.dma_start(out=raw[:].rearrange("p j h c -> p (j h) c"), in_=x_hbm[s])
-            x_raw.append(raw)
+            for h in range(2):
+                x_raw[s, h] = sb.tile([P, PACK, COLS], F32, name="x_raw%d%d" % (s, h), align_bytes=64)
+                nc.sync.dma_start(out=x_raw[s, h][:], in_=x_hbm[s, h])
 
-        own, swapped = [], []
-        for v in range(2):
-            own.append(sb.tile([P, CODE_BYTES + SCALE_BYTES], U8, name="own%d" % v, align_bytes=64))
-            swapped.append(sb.tile([P, CODE_BYTES + SCALE_BYTES], U8, name="swapped%d" % v, align_bytes=64))
+        own = sb.tile([P, WEIGHT_BYTES], U8, name="own", align_bytes=64)
+        swapped = sb.tile([P, WEIGHT_BYTES], U8, name="swapped", align_bytes=64)
 
         zero_bf = sb.tile([P, PACK * COLS], BF16, name="zero_bf", align_bytes=64)
         zero_codes = sb.tile([P, COLS], U32, name="zero_codes", align_bytes=64)
@@ -70,34 +70,32 @@ def tile_rows_pl_dft_pow_kernel(tc, x, fc, fs, out_0, out_1, out_2):
                     stop=True,
                 )
 
-        def window(weights, block, blocks):
-            codes = weights[:, 4 * ROWS * block : 4 * ROWS * (block + blocks)]
-            scales = weights[:, CODE_BYTES + ROWS * block : CODE_BYTES + ROWS * (block + blocks)]
+        def window(weights, u, h, blocks):
+            first_code = BLOCK_BYTES * (2 * u + 1 - h)
+            first_scale = SCALE_START + ROWS * (u - h)
+            codes = weights[:, first_code : first_code + BLOCK_BYTES * blocks]
+            scales = weights[:, first_scale : first_scale + ROWS * blocks]
             return codes, scales
 
         nc.vector.memset(zero_bf[:], 0.0)
         table = sb.tile([P, 1], F32, name="table")
         nc.scalar.activation(out=table[:], in_=zero_bf[:, 0:1], func=ACT.Square)
         nc.vector.quantize_mx(out=zero_codes[:].bitcast(FP8X4), scales=zero_scales[:], in_=zero_bf[:])
-        for v in range(2):
-            nc.vector.memset(own[v][:].bitcast(I32), 0)
+        nc.vector.memset(own[:].bitcast(I32), 0)
+        nc.vector.memset(swapped[:].bitcast(I32), 0)
         warm(WARM_EARLY, zero_codes[:], zero_scales[:])
 
         f_bf = sb.tile([P, PACK, ROWS, PACK], BF16, name="f_bf", align_bytes=64)
-        f_out = f_bf[:].rearrange("p u m j -> p m u j")
-        f_in = f_raw[:].rearrange("p j (m u) -> p m u j", u=PACK)
+        f_out = f_bf[:].rearrange("p u m j -> p m j u")
+        f_in = f_raw[:].rearrange("p j (m u) -> p m j u", u=PACK)
         nc.vector.tensor_copy(out=f_out[:, 0:F_SPLIT], in_=f_in[:, 0:F_SPLIT])
         nc.scalar.activation(out=f_out[:, F_SPLIT:ROWS], in_=f_in[:, F_SPLIT:ROWS], func=ACT.Copy)
         for u in range(PACK):
-            codes, scales = window(own[u // 2], 2 * (u % 2) + 1, 1)
+            codes, scales = window(own, u, 0, 1)
             nc.vector.quantize_mx(
                 out=codes.bitcast(FP8X4), scales=scales, in_=f_bf[:, u].rearrange("p m j -> p (m j)")
             )
-        warm(WARM_LATE, *window(own[0], 0, 2))
-        for v in range(2):
-            nc.sync.dma_start(out=swapped[v][0:ROWS, :].bitcast(I32), in_=own[v][ROWS:P, :].bitcast(I32))
-            nc.sync.dma_start(out=swapped[v][ROWS:P, :].bitcast(I32), in_=own[v][0:ROWS, :].bitcast(I32))
-
+        warm(WARM_LATE, *window(own, 0, 1, 2))
         def interleave(copy, dst, src):
             copy(dst.rearrange("p (c i) t -> p c t i", i=4), src.rearrange("p t (c i) -> p c t i", i=4))
 
@@ -107,57 +105,44 @@ def tile_rows_pl_dft_pow_kernel(tc, x, fc, fs, out_0, out_1, out_2):
         def on_scalar(dst, src):
             nc.scalar.activation(out=dst, in_=src, func=ACT.Copy)
 
-        x_codes, x_scales = {}, {}
+        x_bf, x_codes, x_scales = {}, {}, {}
         for s in range(STEPS):
-            x_bf = []
             for h in range(2):
-                bf = sb.tile([P, COLS, PACK], BF16, name="x_bf%d%d" % (s, h), align_bytes=64)
-                interleave(on_vector if h == 0 else on_scalar, bf[:], x_raw[s][:, :, h, :])
-                x_bf.append(bf)
-            for h in range(2):
+                x_bf[s, h] = sb.tile([P, COLS, PACK], BF16, name="x_bf%d%d" % (s, h), align_bytes=64)
                 x_codes[s, h] = sb.tile([P, COLS], U32, name="x_codes%d%d" % (s, h), align_bytes=64)
                 x_scales[s, h] = sb.tile([P, COLS], U8, name="x_scales%d%d" % (s, h), align_bytes=64)
-                nc.vector.quantize_mx(
-                    out=x_codes[s, h][:].bitcast(FP8X4),
-                    scales=x_scales[s, h][:],
-                    in_=x_bf[h][:].rearrange("p n j -> p (n j)"),
-                )
 
-        banks = {}
-        for s in range(STEPS):
-            for k in range(2):
-                for g in range(G):
-                    if (s, k, g) == (1, 1, 1):
-                        banks[s, k, g] = banks[0, 0, 1]
-                    else:
-                        banks[s, k, g] = ps.tile([P, PACK, COLS], F32, name="bank%d%d%d" % (s, k, g))
+        def round_x(s, h, copy=on_vector, cols=slice(0, COLS)):
+            interleave(copy, x_bf[s, h][:, cols, :], x_raw[s, h][:, :, cols])
 
-        def multiply(s, g, i):
-            k, u, h = i // 8, i // 2 % 4, i % 2
-            codes, scales = window((own, swapped)[k][u // 2], 2 * (u % 2) + 1 - h, 2)
-            rows = slice(ROWS * g, ROWS * (g + 1))
-            nc.tensor.matmul_mx(
-                out=banks[s, k, g][:, u, :],
-                lhsT=codes[rows].bitcast(FP8X4),
-                lhsT_scale=scales[rows],
-                rhs=x_codes[s, h][rows, :].bitcast(FP8X4),
-                rhs_scale=x_scales[s, h][rows, :],
-                start=(h == 0),
-                stop=(h == 1),
+        def quantize_x(s, h):
+            nc.vector.quantize_mx(
+                out=x_codes[s, h][:].bitcast(FP8X4),
+                scales=x_scales[s, h][:],
+                in_=x_bf[s, h][:].rearrange("p n j -> p (n j)"),
             )
 
-        def paired(s):
-            for i in range(16):
-                multiply(s, 0, i)
-                multiply(s, 1, i)
+        round_x(0, 0, on_scalar)
+        low, high = slice(0, ROWS), slice(ROWS, P)
+        for to, source in ((low, high), (high, low)):
+            nc.scalar.dma_start(
+                out=swapped[to, BLOCK_BYTES:].bitcast(I32).rearrange("p (b z w) -> p b z w", z=2, w=ROWS)[:, :, 0, :],
+                in_=own[source, BLOCK_BYTES:].bitcast(I32).rearrange("p (b z w) -> p b z w", z=2, w=ROWS)[:, :, 0, :],
+            )
 
-        def leading(s):
-            for i in range(8):
-                multiply(s, 0, 2 * i)
-                multiply(s, 1, i)
-                multiply(s, 0, 2 * i + 1)
-            for i in range(8, 16):
-                multiply(s, 1, i)
+        round_x(0, 1, on_vector, slice(0, X_SPLIT))
+        round_x(0, 1, on_scalar, slice(X_SPLIT, COLS))
+        quantize_x(0, 0)
+        quantize_x(0, 1)
+        round_x(1, 0)
+        round_x(1, 1)
+        quantize_x(1, 0)
+        quantize_x(1, 1)
+
+        banks = {}
+        for g in range(G):
+            for b in range(BANKS):
+                banks[g, b] = ps.tile([P, PACK, COLS], F32, name="bank%d%d" % (g, b))
 
         squares, ys, y_bf = {}, {}, {}
         words = sb.tile([P, G, STEPS * COLS], U32, name="words", align_bytes=64)
@@ -172,12 +157,30 @@ def tile_rows_pl_dft_pow_kernel(tc, x, fc, fs, out_0, out_1, out_2):
         whole = slice(0, COLS)
         left, right = slice(0, COLS // 2), slice(COLS // 2, COLS)
 
-        def square(s, k, g, cols=whole):
-            nc.scalar.activation(out=squares[s, k, g][:, :, cols], in_=banks[s, k, g][:, :, cols], func=ACT.Square)
+        def multiply_and_square(turn, s, k, a):
+            for slot in range(2):
+                for h in range(2):
+                    codes, scales = window((own, swapped)[k], 2 * a + slot, h, 2)
+                    for g in range(G):
+                        rows = slice(ROWS * g, ROWS * (g + 1))
+                        nc.tensor.matmul_mx(
+                            out=banks[g, turn % BANKS][:, slot, :],
+                            lhsT=codes[rows].bitcast(FP8X4),
+                            lhsT_scale=scales[rows],
+                            rhs=x_codes[s, h][rows, :].bitcast(FP8X4),
+                            rhs_scale=x_scales[s, h][rows, :],
+                            start=(h == 0),
+                            stop=(h == 1),
+                        )
+            for g in range(G):
+                nc.scalar.activation(
+                    out=squares[s, k, g][:, 2 * a : 2 * a + 2, :], in_=banks[g, turn % BANKS][:, 0:2, :], func=ACT.Square
+                )
 
-        def add(s, g, cols=whole):
+        def add(s, g, a):
+            pair = slice(2 * a, 2 * a + 2)
             nc.vector.tensor_tensor(
-                out=ys[s, g][:, :, cols], in0=squares[s, 0, g][:, :, cols], in1=squares[s, 1, g][:, :, cols], op=ADD
+                out=ys[s, g][:, pair, :], in0=squares[s, 0, g][:, pair, :], in1=squares[s, 1, g][:, pair, :], op=ADD
             )
 
         def regroup(s, g, copy=on_vector, cols=whole):
@@ -190,9 +193,13 @@ def tile_rows_pl_dft_pow_kernel(tc, x, fc, fs, out_0, out_1, out_2):
                 in_=y_bf[s, g][:].rearrange("p n u -> p (n u)"),
             )
 
-        def store_y(s, g, h, queue):
-            q = 2 * h + s
-            queue.dma_start(out=y_hbm[g][:, :, COLS * q : COLS * (q + 1)], in_=ys[s, g][ROWS * h : ROWS * (h + 1)])
+        def store_y(s, g, places):
+            for h in range(2):
+                q = 2 * h + s
+                nc.sync.dma_start(
+                    out=y_hbm[g][:, places, COLS * q : COLS * (q + 1)],
+                    in_=ys[s, g][ROWS * h : ROWS * (h + 1), places, :],
+                )
 
         def store_planes(h, queue):
             queue.dma_start(
@@ -206,37 +213,27 @@ def tile_rows_pl_dft_pow_kernel(tc, x, fc, fs, out_0, out_1, out_2):
                     in_=scales[first : first + 4].bitcast(I32),
                 )
 
-        leading(0)
-        square(0, 0, 0)
-        square(0, 1, 0)
-        square(0, 0, 1)
-        add(0, 0)
-        store_y(0, 0, 0, nc.sync)
-        store_y(0, 0, 1, nc.sync)
-        square(0, 1, 1)
-        leading(1)
+        turns = [(0, 0, 0), (0, 0, 1), (0, 1, 0), (0, 1, 1), (1, 0, 0), (1, 1, 0), (1, 0, 1), (1, 1, 1)]
+        for turn, (s, k, a) in enumerate(turns):
+            multiply_and_square(turn, s, k, a)
+
+        add(0, 0, 0)
+        add(0, 1, 0)
+        for g in range(G):
+            add(0, g, 1)
+            store_y(0, g, slice(0, PACK))
         regroup(0, 0)
-        add(0, 1)
-        store_y(0, 1, 0, nc.sync)
-        store_y(0, 1, 1, nc.sync)
-        quantize(0, 0)
         regroup(0, 1)
-        square(1, 0, 0)
-        square(1, 1, 0)
-        add(1, 0)
+        quantize(0, 0)
         quantize(0, 1)
-        store_y(1, 0, 0, nc.sync)
-        store_y(1, 0, 1, nc.sync)
-        square(1, 0, 1)
-        square(1, 1, 1, left)
-        square(1, 1, 1, right)
-        regroup(1, 0, on_scalar)
-        add(1, 1, left)
-        add(1, 1, right)
-        regroup(1, 1, on_vector, left)
-        regroup(1, 1, on_vector, right)
-        store_y(1, 1, 0, nc.sync)
-        store_y(1, 1, 1, nc.scalar)
+        add(1, 0, 0)
+        add(1, 1, 0)
+        for g in range(G):
+            add(1, g, 1)
+            store_y(1, g, slice(0, PACK))
+        regroup(1, 0, on_vector, left)
+        regroup(1, 0, on_scalar, right)
+        regroup(1, 1)
         quantize(1, 0)
         quantize(1, 1)
         store_planes(0, nc.sync)

from contextlib import ExitStack

import concourse.mybir as mybir

G, D, M, N = 2, 256, 256, 512
FLOPS = 2 * 2 * G * D * M * N

F32 = mybir.dt.float32
BF16 = mybir.dt.bfloat16
I32 = mybir.dt.int32
U32 = mybir.dt.uint32
U8 = mybir.dt.uint8
FP8X4 = mybir.dt.float8_e4m3fn_x4
ACT = mybir.ActivationFunctionType
ADD = mybir.AluOpType.add

P = 128
ROWS = 64
PACK = 4
COLS = 128
STEPS = 2
BLOCK_BYTES = 4 * ROWS
SCALE_START = (2 * PACK + 1) * BLOCK_BYTES
WEIGHT_BYTES = SCALE_START + 2 * BLOCK_BYTES
F_SPLIT = 40
X_SPLIT = 88
BANKS = 3
WARM_EARLY = 26
WARM_LATE = 8


def tile_rows_pl_dft_pow_kernel(tc, x, fc, fs, out_0, out_1, out_2):
    nc = tc.nc
    y_hbm = out_0.rearrange("(g p u) n -> g p u n", g=G, u=PACK)
    words_hbm = out_1.rearrange("v p n b -> (v p) (n b)").bitcast(I32).rearrange("(g p) n -> p g n", g=G)
    scales_hbm = out_2.rearrange("v f n -> (v f) n").bitcast(I32).rearrange("(g a r) w -> a r g w", g=G, a=2)
    x_hbm = x.rearrange("g (p j) (h s c) -> s h (g p) j c", j=PACK, h=2, s=STEPS)

    with ExitStack() as ctx:
        sb = ctx.enter_context(tc.tile_pool(name="sb", bufs=1))
        ps = ctx.enter_context(tc.psum_pool(name="ps", bufs=1))
        ctx.enter_context(tc.manual_schedule())

        f_raw = sb.tile([P, PACK, M], F32, name="f_raw", align_bytes=64)
        nc.sync.dma_start(out=f_raw[0:ROWS], in_=fc.rearrange("(p j) m -> p j m", j=PACK))
        nc.scalar.dma_start(out=f_raw[ROWS:P], in_=fs.rearrange("(p j) m -> p j m", j=PACK))
        x_raw = {}
        for s in range(STEPS):
            for h in range(2):
                x_raw[s, h] = sb.tile([P, PACK, COLS], F32, name="x_raw%d%d" % (s, h), align_bytes=64)
                nc.sync.dma_start(out=x_raw[s, h][:], in_=x_hbm[s, h])

        own = sb.tile([P, WEIGHT_BYTES], U8, name="own", align_bytes=64)
        swapped = sb.tile([P, WEIGHT_BYTES], U8, name="swapped", align_bytes=64)

        zero_bf = sb.tile([P, PACK * COLS], BF16, name="zero_bf", align_bytes=64)
        zero_codes = sb.tile([P, COLS], U32, name="zero_codes", align_bytes=64)
        zero_scales = sb.tile([P, COLS], U8, name="zero_scales", align_bytes=64)
        warm_bank = ps.tile([P, COLS], F32, name="warm_bank")

        def warm(count, codes, scales):
            for i in range(count):
                nc.tensor.matmul_mx(
                    out=warm_bank[:],
                    lhsT=codes.bitcast(FP8X4),
                    lhsT_scale=scales,
                    rhs=zero_codes[:].bitcast(FP8X4),
                    rhs_scale=zero_scales[:],
                    start=True,
                    stop=True,
                )

        def window(weights, u, h, blocks):
            first_code = BLOCK_BYTES * (2 * u + 1 - h)
            first_scale = SCALE_START + ROWS * (u - h)
            codes = weights[:, first_code : first_code + BLOCK_BYTES * blocks]
            scales = weights[:, first_scale : first_scale + ROWS * blocks]
            return codes, scales

        nc.vector.memset(zero_bf[:], 0.0)
        table = sb.tile([P, 1], F32, name="table")
        nc.scalar.activation(out=table[:], in_=zero_bf[:, 0:1], func=ACT.Square)
        nc.vector.quantize_mx(out=zero_codes[:].bitcast(FP8X4), scales=zero_scales[:], in_=zero_bf[:])
        nc.vector.memset(own[:].bitcast(I32), 0)
        nc.vector.memset(swapped[:].bitcast(I32), 0)
        warm(WARM_EARLY, zero_codes[:], zero_scales[:])

        f_bf = sb.tile([P, PACK, ROWS, PACK], BF16, name="f_bf", align_bytes=64)
        f_out = f_bf[:].rearrange("p u m j -> p m j u")
        f_in = f_raw[:].rearrange("p j (m u) -> p m j u", u=PACK)
        nc.vector.tensor_copy(out=f_out[:, 0:F_SPLIT], in_=f_in[:, 0:F_SPLIT])
        nc.scalar.activation(out=f_out[:, F_SPLIT:ROWS], in_=f_in[:, F_SPLIT:ROWS], func=ACT.Copy)
        for u in range(PACK):
            codes, scales = window(own, u, 0, 1)
            nc.vector.quantize_mx(
                out=codes.bitcast(FP8X4), scales=scales, in_=f_bf[:, u].rearrange("p m j -> p (m j)")
            )
        warm(WARM_LATE, *window(own, 0, 1, 2))
        def interleave(copy, dst, src):
            copy(dst.rearrange("p (c i) t -> p c t i", i=4), src.rearrange("p t (c i) -> p c t i", i=4))

        def on_vector(dst, src):
            nc.vector.tensor_copy(out=dst, in_=src)

        def on_scalar(dst, src):
            nc.scalar.activation(out=dst, in_=src, func=ACT.Copy)

        x_bf, x_codes, x_scales = {}, {}, {}
        for s in range(STEPS):
            for h in range(2):
                x_bf[s, h] = sb.tile([P, COLS, PACK], BF16, name="x_bf%d%d" % (s, h), align_bytes=64)
                x_codes[s, h] = sb.tile([P, COLS], U32, name="x_codes%d%d" % (s, h), align_bytes=64)
                x_scales[s, h] = sb.tile([P, COLS], U8, name="x_scales%d%d" % (s, h), align_bytes=64)

        def round_x(s, h, copy=on_vector, cols=slice(0, COLS)):
            interleave(copy, x_bf[s, h][:, cols, :], x_raw[s, h][:, :, cols])

        def quantize_x(s, h):
            nc.vector.quantize_mx(
                out=x_codes[s, h][:].bitcast(FP8X4),
                scales=x_scales[s, h][:],
                in_=x_bf[s, h][:].rearrange("p n j -> p (n j)"),
            )

        round_x(0, 0, on_scalar)
        low, high = slice(0, ROWS), slice(ROWS, P)
        for to, source in ((low, high), (high, low)):
            nc.scalar.dma_start(
                out=swapped[to, BLOCK_BYTES:].bitcast(I32).rearrange("p (b z w) -> p b z w", z=2, w=ROWS)[:, :, 0, :],
                in_=own[source, BLOCK_BYTES:].bitcast(I32).rearrange("p (b z w) -> p b z w", z=2, w=ROWS)[:, :, 0, :],
            )

        round_x(0, 1, on_vector, slice(0, X_SPLIT))
        round_x(0, 1, on_scalar, slice(X_SPLIT, COLS))
        quantize_x(0, 0)
        quantize_x(0, 1)
        round_x(1, 0)
        round_x(1, 1)
        quantize_x(1, 0)
        quantize_x(1, 1)

        banks = {}
        for g in range(G):
            for b in range(BANKS):
                banks[g, b] = ps.tile([P, PACK, COLS], F32, name="bank%d%d" % (g, b))

        squares, ys, y_bf = {}, {}, {}
        words = sb.tile([P, G, STEPS * COLS], U32, name="words", align_bytes=64)
        scales = sb.tile([P, G, STEPS * COLS], U8, name="scales", align_bytes=64)
        for s in range(STEPS):
            for g in range(G):
                ys[s, g] = sb.tile([P, PACK, COLS], F32, name="y%d%d" % (s, g), align_bytes=64)
                y_bf[s, g] = sb.tile([P, COLS, PACK], BF16, name="y_bf%d%d" % (s, g), align_bytes=64)
                for k in range(2):
                    squares[s, k, g] = sb.tile([P, PACK, COLS], F32, name="sq%d%d%d" % (s, k, g), align_bytes=64)

        whole = slice(0, COLS)
        left, right = slice(0, COLS // 2), slice(COLS // 2, COLS)

        def multiply_and_square(turn, s, k, a):
            for slot in range(2):
                for h in range(2):
                    codes, scales = window((own, swapped)[k], 2 * a + slot, h, 2)
                    for g in range(G):
                        rows = slice(ROWS * g, ROWS * (g + 1))
                        nc.tensor.matmul_mx(
                            out=banks[g, turn % BANKS][:, slot, :],
                            lhsT=codes[rows].bitcast(FP8X4),
                            lhsT_scale=scales[rows],
                            rhs=x_codes[s, h][rows, :].bitcast(FP8X4),
                            rhs_scale=x_scales[s, h][rows, :],
                            start=(h == 0),
                            stop=(h == 1),
                        )
            for g in range(G):
                nc.scalar.activation(
                    out=squares[s, k, g][:, 2 * a : 2 * a + 2, :], in_=banks[g, turn % BANKS][:, 0:2, :], func=ACT.Square
                )

        def add(s, g, a):
            pair = slice(2 * a, 2 * a + 2)
            nc.vector.tensor_tensor(
                out=ys[s, g][:, pair, :], in0=squares[s, 0, g][:, pair, :], in1=squares[s, 1, g][:, pair, :], op=ADD
            )

        def regroup(s, g, copy=on_vector, cols=whole):
            interleave(copy, y_bf[s, g][:, cols, :], ys[s, g][:, :, cols])

        def quantize(s, g):
            nc.vector.quantize_mx(
                out=words[:, g, COLS * s : COLS * (s + 1)].bitcast(FP8X4),
                scales=scales[:, g, COLS * s : COLS * (s + 1)],
                in_=y_bf[s, g][:].rearrange("p n u -> p (n u)"),
            )

        def store_y(s, g, places):
            for h in range(2):
                q = 2 * h + s
                nc.sync.dma_start(
                    out=y_hbm[g][:, places, COLS * q : COLS * (q + 1)],
                    in_=ys[s, g][ROWS * h : ROWS * (h + 1), places, :],
                )

        def store_planes(h, queue):
            queue.dma_start(
                out=words_hbm[:, :, 2 * COLS * h : 2 * COLS * (h + 1)],
                in_=words[ROWS * h : ROWS * (h + 1)].bitcast(I32),
            )
            for a in range(2):
                first = ROWS * h + 32 * a
                queue.dma_start(
                    out=scales_hbm[a][:, :, 64 * h : 64 * (h + 1)],
                    in_=scales[first : first + 4].bitcast(I32),
                )

        turns = [(0, 0, 0), (0, 0, 1), (0, 1, 0), (0, 1, 1), (1, 0, 0), (1, 1, 0), (1, 0, 1), (1, 1, 1)]
        for turn, (s, k, a) in enumerate(turns):
            multiply_and_square(turn, s, k, a)

        add(0, 0, 0)
        add(0, 1, 0)
        for g in range(G):
            add(0, g, 1)
            store_y(0, g, slice(0, PACK))
        regroup(0, 0)
        regroup(0, 1)
        quantize(0, 0)
        quantize(0, 1)
        add(1, 0, 0)
        add(1, 1, 0)
        for g in range(G):
            add(1, g, 1)
            store_y(1, g, slice(0, PACK))
        regroup(1, 0, on_vector, left)
        regroup(1, 0, on_scalar, right)
        regroup(1, 1)
        quantize(1, 0)
        quantize(1, 1)
        store_planes(0, nc.sync)
        store_planes(1, nc.scalar)
